import numpy as np, ml_dtypes
CORES = [16,23,24,31,64,71]
N = 6
import mx_ref
NC, G, D = 128, 2, 2
C = np.float32(0.041)
BF = ml_dtypes.bfloat16
def cut(t, i, w=512):
    return t[:, w * i:w * i + w]
def tile(rs):
    return np.stack(rs, axis=2).reshape(128, -1).astype(BF)
def act(Z):
    return [np.maximum(s * z, 0) * C for z in Z for s in (1, -1)]
def taps(w, i, e):
    return mx_ref.matmul(mx_ref.quantize(cut(w, 2 * i)), mx_ref.quantize(e[:, :4 * NC])) + mx_ref.matmul(mx_ref.quantize(cut(w, 2 * i + 1)), mx_ref.quantize(e[:, 4 * D:4 * D + 4 * NC]))
def setup_inputs(rng):
    def f(*shape):
        return mx_ref.flush((rng.standard_normal(shape, dtype=np.float32) * np.exp2(rng.integers(-2, 3, shape[:-1] + (1,)))).astype(BF))
    return {"x": f(N, 128, 4 * NC), "wa": np.broadcast_to(f(1, 128, 2 * G * 512), (N, 128, 2 * G * 512)).copy(), "wb": f(N, 128, 2 * 512)}
def setup_inputs_blocks(rng):
    d = setup_inputs(rng)
    for k in ("x", "wb"): d[k] = mx_ref.spread(d[k], rng, 2)
    return d
def setup_inputs_wide(rng):
    d = setup_inputs(rng)
    for k in ("wb",): d[k] = mx_ref.flush((d[k].astype(np.float32) * np.exp2(rng.integers(-6, 7, (N, 1, 1))).astype(np.float32)).astype(BF))
    return d
def setup_inputs_zeros(rng):
    d = setup_inputs(rng); v = d["x"].reshape(N, 128, -1, 4).copy()
    v[np.broadcast_to((rng.random((N, 1, v.shape[2], 1)) < 0.33), v.shape)] = 0
    d["x"] = v.reshape(d["x"].shape)
    return d
def reference(x, wa, wb):
    edge = lambda t, r: np.concatenate([t[(r - 1) % N][:, 4 * (NC - D):], t[r]], axis=1)
    u = [tile(act([taps(wa[r], i, edge(x, r)) for i in range(G)])) for r in range(N)]
    y = np.zeros((N, 128, NC), np.float32)
    for r in range(N):
        y[r] = taps(wb[r], 0, edge(u, r))
    return {"y": y}

@@ -1,0 +1,122 @@
+import numpy as np
+from concourse.mybir import dt, AluOpType, ActivationFunctionType
+
+C = float(np.float32(0.041))
+H = 4
+NC = 128
+B0 = 16
+ENGINES = 4
+
+SCRATCH = {
+    "xt": ("sbuf", [128, 512], "bfloat16"),
+    "xq": ("sbuf", [128, 272], "float8_e4m3fn_x4"), "xs": ("sbuf", [128, 272], "uint8"),
+    "at": ("sbuf", [128, 2048], "bfloat16"),
+    "aq": ("sbuf", [128, 512], "float8_e4m3fn_x4"), "as_": ("sbuf", [128, 512], "uint8"),
+    "bt": ("sbuf", [128, 1024], "bfloat16"),
+    "bq": ("sbuf", [128, 256], "float8_e4m3fn_x4"), "bs": ("sbuf", [128, 256], "uint8"),
+    "ut": ("sbuf", [128, 536], "bfloat16"),
+    "uq": ("sbuf", [128, 130], "float8_e4m3fn_x4"), "us": ("sbuf", [128, 130], "uint8"),
+    "vq": ("sbuf", [128, 130], "float8_e4m3fn_x4"), "vs": ("sbuf", [128, 130], "uint8"),
+    "yi": ("sbuf", [128, 124], "float32"), "ye": ("sbuf", [128, 4], "float32"),
+    "pzi": ("psum", [128, 1024], "float32"), "pze": ("psum", [128, 1024], "float32"),
+    "pyi": ("psum", [128, 512], "float32"), "pye": ("psum", [128, 512], "float32"),
+}
+SEMAPHORES = ["fill", "ld_x", "ld_a0", "ld_a1", "ld_b", "q_x", "q_x2", "q_a0", "q_a1", "q_b", "q_u", "q_v",
+              "m_i0", "m_i1", "m_e0", "m_e1", "m_yi", "m_ye", "a_i", "a_e", "c_i", "c_e", "st_i", "st_e",
+              "sent", "arrived"]
+
+
+def engines(topo, src, dst):
+    m = topo.mask(src, dst)
+    bits = [b for b in range(m.bit_length()) if (m >> b) & 1]
+    pick = bits[::len(bits) // ENGINES]
+    return sum(1 << b for b in pick), len(pick)
+
+
+def rank_program(g, core, T, topo):
+    rank = T.rank_of(core)
+    if rank is None:
+        return
+    n = len(T.cores)
+    prv, nxt = T.cores[(rank - 1) % n], T.cores[(rank + 1) % n]
+    S, V, P, A, D = T.sem, g.vector, g.tensor, g.scalar, g.sync
+    Relu, Copy = ActivationFunctionType.Relu, ActivationFunctionType.Copy
+
+    D.dma_start(T.xt[:], T.x[:, :]).then_inc(S.ld_x, 16)
+    D.dma_start(T.at[:, 0:1024], T.wa[:, 0:1024]).then_inc(S.ld_a0, 16)
+    D.dma_start(T.at[:, 1024:2048], T.wa[:, 1024:2048]).then_inc(S.ld_a1, 16)
+    D.dma_start(T.bt[:], T.wb[:, :]).then_inc(S.ld_b, 16)
+
+    rid, pid, _se = topo.addr(nxt)
+    mask, k = engines(topo, core, nxt)
+    g.wait_ge(S.q_x, 1)
+    g.remote_dma(T.xq[:, B0 - H:B0].bitcast(dt.uint8), T.xq[:, B0 + NC - H:B0 + NC].bitcast(dt.uint8),
+                 S.arrived, S.sent, pid, rid, mask)
+    g.remote_dma(T.xs[:, B0 - H:B0], T.xs[:, B0 + NC - H:B0 + NC], S.arrived, S.sent, pid, rid, mask)
+    g.wait_ge(S.sent, 2 * k)
+
+    V.memset(T.ut[:, 520:536], 0.0).then_inc(S.fill, 1)
+    V.wait_ge(S.fill, 1)
+    V.wait_ge(S.ld_x, 16)
+    V.quantize_mx(T.xq[:, B0:B0 + NC], T.xs[:, B0:B0 + NC], T.xt[:]).then_inc(S.q_x, 1)
+    V.quantize_mx(T.xq[:, B0 + NC:B0 + 2 * NC], T.xs[:, B0 + NC:B0 + 2 * NC], T.xt[:]).then_inc(S.q_x2, 1)
+    V.wait_ge(S.ld_a0, 16)
+    V.quantize_mx(T.aq[:, 0:256], T.as_[:, 0:256], T.at[:, 0:1024]).then_inc(S.q_a0, 1)
+    V.wait_ge(S.ld_a1, 16)
+    V.quantize_mx(T.aq[:, 256:512], T.as_[:, 256:512], T.at[:, 1024:2048]).then_inc(S.q_a1, 1)
+    V.wait_ge(S.ld_b, 16)
+    V.quantize_mx(T.bq[:], T.bs[:], T.bt[:]).then_inc(S.q_b, 1)
+
+    def wa(i, t):
+        c = 128 * (2 * i + t)
+        return T.aq[:, c:c + 128], T.as_[:, c:c + 128]
+
+    def wb(t):
+        return T.bq[:, 128 * t:128 * t + 128], T.bs[:, 128 * t:128 * t + 128]
+
+    def layer(out, w, q, s, c, done):
+        for t in (0, 1):
+            a, b = c + 2 * t, c + 2 * t + NC
+            ins = P.matmul_mx(out, w(t)[0], w(t)[1], q[:, a:b], s[:, a:b], t == 0, t == 1)
+        ins.then_inc(done, 1)
+
+    P.wait_ge(S.q_x, 1)
+    P.wait_ge(S.q_x2, 1)
+    P.wait_ge(S.q_a0, 1)
+    layer(T.pzi[:, 0:128], lambda t: wa(0, t), T.xq, T.xs, B0, S.m_i0)
+    P.wait_ge(S.q_a1, 1)
+    layer(T.pzi[:, 512:640], lambda t: wa(1, t), T.xq, T.xs, B0, S.m_i1)
+    P.wait_ge(S.q_b, 1)
+    P.wait_ge(S.q_u, 1)
+    layer(T.pyi[:, 0:128], wb, T.uq, T.us, 0, S.m_yi)
+    P.wait_ge(S.arrived, 2 * engines(topo, prv, core)[1])
+    layer(T.pze[:, 0:128], lambda t: wa(0, t), T.xq, T.xs, B0 - H, S.m_e0)
+    layer(T.pze[:, 512:640], lambda t: wa(1, t), T.xq, T.xs, B0 - H, S.m_e1)
+    P.wait_ge(S.q_v, 1)
+    layer(T.pye[:, 0:128], wb, T.vq, T.vs, 0, S.m_ye)
+
+    for i, done in ((0, S.m_i0), (1, S.m_i1)):
+        A.wait_ge(done, 1)
+        for b, c in ((2 * i, C), (2 * i + 1, -C)):
+            A.activation(T.ut[:, 16 + b:520:4], T.pzi[:, 512 * i:512 * i + 126], Relu, scale=c).then_inc(S.a_i, 1)
+    A.wait_ge(S.m_yi, 1)
+    A.activation(T.yi[:], T.pyi[:, 0:124], Copy).then_inc(S.c_i, 1)
+    A.wait_ge(S.c_i, 1)
+    A.dma_start(T.y[:, 4:128], T.yi[:]).then_inc(S.st_i, 16)
+    A.wait_ge(S.st_i, 16)
+
+    V.wait_ge(S.a_i, 4)
+    V.quantize_mx(T.uq[:], T.us[:], T.ut[:, 16:536]).then_inc(S.q_u, 1)
+    for i, done in ((0, S.m_e0), (1, S.m_e1)):
+        V.wait_ge(done, 1)
+        z = T.pze[:, 512 * i:512 * i + 4]
+        V.tensor_scalar(T.ut[:, 2 * i:16:4], z, 0.0, C, AluOpType.max, AluOpType.mult).then_inc(S.a_e, 1)
+        V.tensor_scalar(T.ut[:, 2 * i + 1:16:4], z, -C, 0.0, AluOpType.mult, AluOpType.max).then_inc(S.a_e, 1)
+    V.wait_ge(S.a_e, 4)
+    V.quantize_mx(T.vq[:], T.vs[:], T.ut[:, 0:520]).then_inc(S.q_v, 1)
+    V.wait_ge(S.m_ye, 1)
+    V.tensor_copy(T.ye[:], T.pye[:, 0:4]).then_inc(S.c_e, 1)
+
+    D.wait_ge(S.c_e, 1)
+    D.dma_start(T.y[:, 0:4], T.ye[:]).then_inc(S.st_e, 16)
+    D.wait_ge(S.st_e, 16)

@@ -2,10 +2,10 @@ import numpy as np
 from concourse.mybir import dt, AluOpType, ActivationFunctionType
 
 C = float(np.float32(0.041))
-H = 4
+H = 2
 NC = 128
 B0 = 16
-ENGINES = 4
+ENGINES = 8
 
 SCRATCH = {
     "xt": ("sbuf", [128, 512], "bfloat16"),
@@ -14,16 +14,18 @@ SCRATCH = {
     "aq": ("sbuf", [128, 512], "float8_e4m3fn_x4"), "as_": ("sbuf", [128, 512], "uint8"),
     "bt": ("sbuf", [128, 1024], "bfloat16"),
     "bq": ("sbuf", [128, 256], "float8_e4m3fn_x4"), "bs": ("sbuf", [128, 256], "uint8"),
-    "ut": ("sbuf", [128, 536], "bfloat16"),
+    "et": ("sbuf", [128, 512], "bfloat16"),
+    "eq": ("sbuf", [128, 128], "float8_e4m3fn_x4"), "es": ("sbuf", [128, 128], "uint8"),
+    "ut": ("sbuf", [128, 528], "bfloat16"),
     "uq": ("sbuf", [128, 130], "float8_e4m3fn_x4"), "us": ("sbuf", [128, 130], "uint8"),
-    "vq": ("sbuf", [128, 130], "float8_e4m3fn_x4"), "vs": ("sbuf", [128, 130], "uint8"),
+    "vq": ("sbuf", [128, 144], "float8_e4m3fn_x4"), "vs": ("sbuf", [128, 144], "uint8"),
     "yi": ("sbuf", [128, 124], "float32"), "ye": ("sbuf", [128, 4], "float32"),
     "pzi": ("psum", [128, 1024], "float32"), "pze": ("psum", [128, 1024], "float32"),
     "pyi": ("psum", [128, 512], "float32"), "pye": ("psum", [128, 512], "float32"),
 }
-SEMAPHORES = ["fill", "ld_x", "ld_a0", "ld_a1", "ld_b", "q_x", "q_x2", "q_a0", "q_a1", "q_b", "q_u", "q_v",
-              "m_i0", "m_i1", "m_e0", "m_e1", "m_yi", "m_ye", "a_i", "a_e", "c_i", "c_e", "st_i", "st_e",
-              "sent", "arrived"]
+SEMAPHORES = ["fill", "ld_x", "ld_a0", "ld_a2", "ld_a3", "ld_b", "q_x", "q_x2", "q_a0", "q_a1", "q_a2", "q_a3", "q_b",
+              "q_w", "q_u", "q_v", "m_i0", "m_i1", "m_e0", "m_e1", "m_yi", "m_ye", "a_w0", "a_w1", "a_i", "a_e",
+              "c_i", "c_e", "st_i", "st_e", "sent", "arr_x", "arr_u"]
 
 
 def engines(topo, src, dst):
@@ -44,26 +46,42 @@ def rank_program(g, core, T, topo):
 
     D.dma_start(T.xt[:], T.x[:, :]).then_inc(S.ld_x, 16)
     D.dma_start(T.at[:, 0:1024], T.wa[:, 0:1024]).then_inc(S.ld_a0, 16)
-    D.dma_start(T.at[:, 1024:2048], T.wa[:, 1024:2048]).then_inc(S.ld_a1, 16)
+    D.dma_start(T.at[:, 1024:1536], T.wa[:, 1024:1536]).then_inc(S.ld_a2, 16)
+    D.dma_start(T.at[:, 1536:2048], T.wa[:, 1536:2048]).then_inc(S.ld_a3, 16)
     D.dma_start(T.bt[:], T.wb[:, :]).then_inc(S.ld_b, 16)
 
     rid, pid, _se = topo.addr(nxt)
     mask, k = engines(topo, core, nxt)
+    ka = engines(topo, prv, core)[1]
     g.wait_ge(S.q_x, 1)
     g.remote_dma(T.xq[:, B0 - H:B0].bitcast(dt.uint8), T.xq[:, B0 + NC - H:B0 + NC].bitcast(dt.uint8),
-                 S.arrived, S.sent, pid, rid, mask)
-    g.remote_dma(T.xs[:, B0 - H:B0], T.xs[:, B0 + NC - H:B0 + NC], S.arrived, S.sent, pid, rid, mask)
-    g.wait_ge(S.sent, 2 * k)
+                 S.arr_x, S.sent, pid, rid, mask)
+    g.remote_dma(T.xs[:, B0 - H:B0], T.xs[:, B0 + NC - H:B0 + NC], S.arr_x, S.sent, pid, rid, mask)
+    g.wait_ge(S.q_w, 1)
+    g.remote_dma(T.vq[:, B0 - H:B0].bitcast(dt.uint8), T.eq[:, 0:H].bitcast(dt.uint8), S.arr_u, S.sent, pid, rid, mask)
+    g.remote_dma(T.vs[:, B0 - H:B0], T.es[:, 0:H], S.arr_u, S.sent, pid, rid, mask)
+    g.wait_ge(S.sent, 4 * k)
 
-    V.memset(T.ut[:, 520:536], 0.0).then_inc(S.fill, 1)
-    V.wait_ge(S.fill, 1)
+    V.memset(T.ut[:, 512:528], 0.0).then_inc(S.fill, 1)
+    V.memset(T.et[:, 8:512], 0.0).then_inc(S.fill, 1)
+    V.wait_ge(S.fill, 2)
     V.wait_ge(S.ld_x, 16)
     V.quantize_mx(T.xq[:, B0:B0 + NC], T.xs[:, B0:B0 + NC], T.xt[:]).then_inc(S.q_x, 1)
     V.quantize_mx(T.xq[:, B0 + NC:B0 + 2 * NC], T.xs[:, B0 + NC:B0 + 2 * NC], T.xt[:]).then_inc(S.q_x2, 1)
-    V.wait_ge(S.ld_a0, 16)
-    V.quantize_mx(T.aq[:, 0:256], T.as_[:, 0:256], T.at[:, 0:1024]).then_inc(S.q_a0, 1)
-    V.wait_ge(S.ld_a1, 16)
-    V.quantize_mx(T.aq[:, 256:512], T.as_[:, 256:512], T.at[:, 1024:2048]).then_inc(S.q_a1, 1)
+    for t, load, done in ((0, S.ld_a0, S.q_a0), (1, None, S.q_a1), (2, S.ld_a2, S.q_a2), (3, S.ld_a3, S.q_a3)):
+        if load is not None:
+            V.wait_ge(load, 16)
+        V.quantize_mx(T.aq[:, 128 * t:128 * t + 128], T.as_[:, 128 * t:128 * t + 128],
+                      T.at[:, 512 * t:512 * t + 512]).then_inc(done, 1)
+
+    for i, done, made in ((0, S.m_i0, S.a_w0), (1, S.m_i1, S.a_w1)):
+        V.wait_ge(done, 1)
+        z = T.pzi[:, 512 * i + 124:512 * i + 126]
+        V.tensor_scalar(T.et[:, 2 * i:8:4], z, 0.0, C, AluOpType.max, AluOpType.mult).then_inc(made, 1)
+        V.tensor_scalar(T.et[:, 2 * i + 1:8:4], z, -C, 0.0, AluOpType.mult, AluOpType.max).then_inc(made, 1)
+    V.wait_ge(S.a_w0, 2)
+    V.wait_ge(S.a_w1, 2)
+    V.quantize_mx(T.eq[:], T.es[:], T.et[:]).then_inc(S.q_w, 1)
     V.wait_ge(S.ld_b, 16)
     V.quantize_mx(T.bq[:], T.bs[:], T.bt[:]).then_inc(S.q_b, 1)
 
@@ -74,31 +92,38 @@ def rank_program(g, core, T, topo):
     def wb(t):
         return T.bq[:, 128 * t:128 * t + 128], T.bs[:, 128 * t:128 * t + 128]
 
-    def layer(out, w, q, s, c, done):
-        for t in (0, 1):
-            a, b = c + 2 * t, c + 2 * t + NC
-            ins = P.matmul_mx(out, w(t)[0], w(t)[1], q[:, a:b], s[:, a:b], t == 0, t == 1)
-        ins.then_inc(done, 1)
+    def mm(out, w, q, s, c, start, stop):
+        return P.matmul_mx(out, w[0], w[1], q[:, c:c + NC], s[:, c:c + NC], start, stop)
 
+    Z0, Z1, E0, E1 = T.pzi[:, 0:128], T.pzi[:, 512:640], T.pze[:, 0:128], T.pze[:, 512:640]
     P.wait_ge(S.q_x, 1)
     P.wait_ge(S.q_x2, 1)
     P.wait_ge(S.q_a0, 1)
-    layer(T.pzi[:, 0:128], lambda t: wa(0, t), T.xq, T.xs, B0, S.m_i0)
+    mm(Z0, wa(0, 0), T.xq, T.xs, B0, True, False)
     P.wait_ge(S.q_a1, 1)
-    layer(T.pzi[:, 512:640], lambda t: wa(1, t), T.xq, T.xs, B0, S.m_i1)
+    mm(Z0, wa(0, 1), T.xq, T.xs, B0 + 2, False, True).then_inc(S.m_i0, 1)
+    P.wait_ge(S.q_a2, 1)
+    mm(Z1, wa(1, 0), T.xq, T.xs, B0, True, False)
+    P.wait_ge(S.q_a3, 1)
+    mm(Z1, wa(1, 1), T.xq, T.xs, B0 + 2, False, True).then_inc(S.m_i1, 1)
+    mm(E0, wa(0, 1), T.xq, T.xs, B0, True, False)
+    mm(E1, wa(1, 1), T.xq, T.xs, B0, True, False)
+    P.wait_ge(S.arr_x, 2 * ka)
+    mm(E0, wa(0, 0), T.xq, T.xs, B0 - 2, False, True).then_inc(S.m_e0, 1)
+    mm(E1, wa(1, 0), T.xq, T.xs, B0 - 2, False, True).then_inc(S.m_e1, 1)
     P.wait_ge(S.q_b, 1)
     P.wait_ge(S.q_u, 1)
-    layer(T.pyi[:, 0:128], wb, T.uq, T.us, 0, S.m_yi)
-    P.wait_ge(S.arrived, 2 * engines(topo, prv, core)[1])
-    layer(T.pze[:, 0:128], lambda t: wa(0, t), T.xq, T.xs, B0 - H, S.m_e0)
-    layer(T.pze[:, 512:640], lambda t: wa(1, t), T.xq, T.xs, B0 - H, S.m_e1)
+    mm(T.pyi[:, 0:128], wb(0), T.uq, T.us, 0, True, False)
+    mm(T.pyi[:, 0:128], wb(1), T.uq, T.us, 2, False, True).then_inc(S.m_yi, 1)
     P.wait_ge(S.q_v, 1)
-    layer(T.pye[:, 0:128], wb, T.vq, T.vs, 0, S.m_ye)
+    mm(T.pye[:, 0:128], wb(1), T.vq, T.vs, B0, True, False)
+    P.wait_ge(S.arr_u, 2 * ka)
+    mm(T.pye[:, 0:128], wb(0), T.vq, T.vs, B0 - 2, False, True).then_inc(S.m_ye, 1)
 
-    for i, done in ((0, S.m_i0), (1, S.m_i1)):
-        A.wait_ge(done, 1)
+    for i, made in ((0, S.a_w0), (1, S.a_w1)):
+        A.wait_ge(made, 2)
         for b, c in ((2 * i, C), (2 * i + 1, -C)):
-            A.activation(T.ut[:, 16 + b:520:4], T.pzi[:, 512 * i:512 * i + 126], Relu, scale=c).then_inc(S.a_i, 1)
+            A.activation(T.ut[:, 8 + b:512:4], T.pzi[:, 512 * i:512 * i + 126], Relu, scale=c).then_inc(S.a_i, 1)
     A.wait_ge(S.m_yi, 1)
     A.activation(T.yi[:], T.pyi[:, 0:124], Copy).then_inc(S.c_i, 1)
     A.wait_ge(S.c_i, 1)
@@ -106,14 +131,14 @@ def rank_program(g, core, T, topo):
     A.wait_ge(S.st_i, 16)
 
     V.wait_ge(S.a_i, 4)
-    V.quantize_mx(T.uq[:], T.us[:], T.ut[:, 16:536]).then_inc(S.q_u, 1)
+    V.quantize_mx(T.uq[:], T.us[:], T.ut[:, 8:528]).then_inc(S.q_u, 1)
     for i, done in ((0, S.m_e0), (1, S.m_e1)):
         V.wait_ge(done, 1)
-        z = T.pze[:, 512 * i:512 * i + 4]
-        V.tensor_scalar(T.ut[:, 2 * i:16:4], z, 0.0, C, AluOpType.max, AluOpType.mult).then_inc(S.a_e, 1)
-        V.tensor_scalar(T.ut[:, 2 * i + 1:16:4], z, -C, 0.0, AluOpType.mult, AluOpType.max).then_inc(S.a_e, 1)
+        z = T.pze[:, 512 * i:512 * i + 2]
+        V.tensor_scalar(T.ut[:, 2 * i:8:4], z, 0.0, C, AluOpType.max, AluOpType.mult).then_inc(S.a_e, 1)
+        V.tensor_scalar(T.ut[:, 2 * i + 1:8:4], z, -C, 0.0, AluOpType.mult, AluOpType.max).then_inc(S.a_e, 1)
     V.wait_ge(S.a_e, 4)
-    V.quantize_mx(T.vq[:], T.vs[:], T.ut[:, 0:520]).then_inc(S.q_v, 1)
+    V.quantize_mx(T.vq[:, B0:B0 + NC], T.vs[:, B0:B0 + NC], T.ut[:, 0:512]).then_inc(S.q_v, 1)
     V.wait_ge(S.m_ye, 1)
     V.tensor_copy(T.ye[:], T.pye[:, 0:4]).then_inc(S.c_e, 1)
 

import numpy as np
from concourse.mybir import dt, AluOpType, ActivationFunctionType

C = float(np.float32(0.041))
H = 2
NC = 128
B0 = 16
ENGINES = 8

SCRATCH = {
    "xt": ("sbuf", [128, 512], "bfloat16"),
    "xq": ("sbuf", [128, 272], "float8_e4m3fn_x4"), "xs": ("sbuf", [128, 272], "uint8"),
    "at": ("sbuf", [128, 2048], "bfloat16"),
    "aq": ("sbuf", [128, 512], "float8_e4m3fn_x4"), "as_": ("sbuf", [128, 512], "uint8"),
    "bt": ("sbuf", [128, 1024], "bfloat16"),
    "bq": ("sbuf", [128, 256], "float8_e4m3fn_x4"), "bs": ("sbuf", [128, 256], "uint8"),
    "et": ("sbuf", [128, 512], "bfloat16"),
    "eq": ("sbuf", [128, 128], "float8_e4m3fn_x4"), "es": ("sbuf", [128, 128], "uint8"),
    "ut": ("sbuf", [128, 528], "bfloat16"),
    "uq": ("sbuf", [128, 130], "float8_e4m3fn_x4"), "us": ("sbuf", [128, 130], "uint8"),
    "vq": ("sbuf", [128, 144], "float8_e4m3fn_x4"), "vs": ("sbuf", [128, 144], "uint8"),
    "yi": ("sbuf", [128, 124], "float32"), "ye": ("sbuf", [128, 4], "float32"),
    "pzi": ("psum", [128, 1024], "float32"), "pze": ("psum", [128, 1024], "float32"),
    "pyi": ("psum", [128, 512], "float32"), "pye": ("psum", [128, 512], "float32"),
}
SEMAPHORES = ["fill", "ld_x", "ld_a0", "ld_a2", "ld_a3", "ld_b", "q_x", "q_x2", "q_a0", "q_a1", "q_a2", "q_a3", "q_b",
              "q_w", "q_u", "q_v", "m_i0", "m_i1", "m_e0", "m_e1", "m_yi", "m_ye", "a_w0", "a_w1", "a_i", "a_e",
              "c_i", "c_e", "st_i", "st_e", "sent", "arr_x", "arr_u"]


def engines(topo, src, dst):
    m = topo.mask(src, dst)
    bits = [b for b in range(m.bit_length()) if (m >> b) & 1]
    pick = bits[::len(bits) // ENGINES]
    return sum(1 << b for b in pick), len(pick)


def rank_program(g, core, T, topo):
    rank = T.rank_of(core)
    if rank is None:
        return
    n = len(T.cores)
    prv, nxt = T.cores[(rank - 1) % n], T.cores[(rank + 1) % n]
    S, V, P, A, D = T.sem, g.vector, g.tensor, g.scalar, g.sync
    Relu, Copy = ActivationFunctionType.Relu, ActivationFunctionType.Copy

    D.dma_start(T.xt[:], T.x[:, :]).then_inc(S.ld_x, 16)
    D.dma_start(T.at[:, 0:1024], T.wa[:, 0:1024]).then_inc(S.ld_a0, 16)
    D.dma_start(T.at[:, 1024:1536], T.wa[:, 1024:1536]).then_inc(S.ld_a2, 16)
    D.dma_start(T.at[:, 1536:2048], T.wa[:, 1536:2048]).then_inc(S.ld_a3, 16)
    D.dma_start(T.bt[:], T.wb[:, :]).then_inc(S.ld_b, 16)

    rid, pid, _se = topo.addr(nxt)
    mask, k = engines(topo, core, nxt)
    ka = engines(topo, prv, core)[1]
    g.wait_ge(S.q_x, 1)
    g.remote_dma(T.xq[:, B0 - H:B0].bitcast(dt.uint8), T.xq[:, B0 + NC - H:B0 + NC].bitcast(dt.uint8),
                 S.arr_x, S.sent, pid, rid, mask)
    g.remote_dma(T.xs[:, B0 - H:B0], T.xs[:, B0 + NC - H:B0 + NC], S.arr_x, S.sent, pid, rid, mask)
    g.wait_ge(S.q_w, 1)
    g.remote_dma(T.vq[:, B0 - H:B0].bitcast(dt.uint8), T.eq[:, 0:H].bitcast(dt.uint8), S.arr_u, S.sent, pid, rid, mask)
    g.remote_dma(T.vs[:, B0 - H:B0], T.es[:, 0:H], S.arr_u, S.sent, pid, rid, mask)
    g.wait_ge(S.sent, 4 * k)

    V.memset(T.ut[:, 512:528], 0.0).then_inc(S.fill, 1)
    V.memset(T.et[:, 8:512], 0.0).then_inc(S.fill, 1)
    V.wait_ge(S.fill, 2)
    V.wait_ge(S.ld_x, 16)
    V.quantize_mx(T.xq[:, B0:B0 + NC], T.xs[:, B0:B0 + NC], T.xt[:]).then_inc(S.q_x, 1)
    V.quantize_mx(T.xq[:, B0 + NC:B0 + 2 * NC], T.xs[:, B0 + NC:B0 + 2 * NC], T.xt[:]).then_inc(S.q_x2, 1)
    for t, load, done in ((0, S.ld_a0, S.q_a0), (1, None, S.q_a1), (2, S.ld_a2, S.q_a2), (3, S.ld_a3, S.q_a3)):
        if load is not None:
            V.wait_ge(load, 16)
        V.quantize_mx(T.aq[:, 128 * t:128 * t + 128], T.as_[:, 128 * t:128 * t + 128],
                      T.at[:, 512 * t:512 * t + 512]).then_inc(done, 1)

    for i, done, made in ((0, S.m_i0, S.a_w0), (1, S.m_i1, S.a_w1)):
        V.wait_ge(done, 1)
        z = T.pzi[:, 512 * i + 124:512 * i + 126]
        V.tensor_scalar(T.et[:, 2 * i:8:4], z, 0.0, C, AluOpType.max, AluOpType.mult).then_inc(made, 1)
        V.tensor_scalar(T.et[:, 2 * i + 1:8:4], z, -C, 0.0, AluOpType.mult, AluOpType.max).then_inc(made, 1)
    V.wait_ge(S.a_w0, 2)
    V.wait_ge(S.a_w1, 2)
    V.quantize_mx(T.eq[:], T.es[:], T.et[:]).then_inc(S.q_w, 1)
    V.wait_ge(S.ld_b, 16)
    V.quantize_mx(T.bq[:], T.bs[:], T.bt[:]).then_inc(S.q_b, 1)

    def wa(i, t):
        c = 128 * (2 * i + t)
        return T.aq[:, c:c + 128], T.as_[:, c:c + 128]

    def wb(t):
        return T.bq[:, 128 * t:128 * t + 128], T.bs[:, 128 * t:128 * t + 128]

    def mm(out, w, q, s, c, start, stop):
        return P.matmul_mx(out, w[0], w[1], q[:, c:c + NC], s[:, c:c + NC], start, stop)

    Z0, Z1, E0, E1 = T.pzi[:, 0:128], T.pzi[:, 512:640], T.pze[:, 0:128], T.pze[:, 512:640]
    P.wait_ge(S.q_x, 1)
    P.wait_ge(S.q_x2, 1)
    P.wait_ge(S.q_a0, 1)
    mm(Z0, wa(0, 0), T.xq, T.xs, B0, True, False)
    P.wait_ge(S.q_a1, 1)
    mm(Z0, wa(0, 1), T.xq, T.xs, B0 + 2, False, True).then_inc(S.m_i0, 1)
    P.wait_ge(S.q_a2, 1)
    mm(Z1, wa(1, 0), T.xq, T.xs, B0, True, False)
    P.wait_ge(S.q_a3, 1)
    mm(Z1, wa(1, 1), T.xq, T.xs, B0 + 2, False, True).then_inc(S.m_i1, 1)
    mm(E0, wa(0, 1), T.xq, T.xs, B0, True, False)
    mm(E1, wa(1, 1), T.xq, T.xs, B0, True, False)
    P.wait_ge(S.arr_x, 2 * ka)
    mm(E0, wa(0, 0), T.xq, T.xs, B0 - 2, False, True).then_inc(S.m_e0, 1)
    mm(E1, wa(1, 0), T.xq, T.xs, B0 - 2, False, True).then_inc(S.m_e1, 1)
    P.wait_ge(S.q_b, 1)
    P.wait_ge(S.q_u, 1)
    mm(T.pyi[:, 0:128], wb(0), T.uq, T.us, 0, True, False)
    mm(T.pyi[:, 0:128], wb(1), T.uq, T.us, 2, False, True).then_inc(S.m_yi, 1)
    P.wait_ge(S.q_v, 1)
    mm(T.pye[:, 0:128], wb(1), T.vq, T.vs, B0, True, False)
    P.wait_ge(S.arr_u, 2 * ka)
    mm(T.pye[:, 0:128], wb(0), T.vq, T.vs, B0 - 2, False, True).then_inc(S.m_ye, 1)

    for i, made in ((0, S.a_w0), (1, S.a_w1)):
        A.wait_ge(made, 2)
        for b, c in ((2 * i, C), (2 * i + 1, -C)):
            A.activation(T.ut[:, 8 + b:512:4], T.pzi[:, 512 * i:512 * i + 126], Relu, scale=c).then_inc(S.a_i, 1)
    A.wait_ge(S.m_yi, 1)
    A.activation(T.yi[:], T.pyi[:, 0:124], Copy).then_inc(S.c_i, 1)
    A.wait_ge(S.c_i, 1)
    A.dma_start(T.y[:, 4:128], T.yi[:]).then_inc(S.st_i, 16)
    A.wait_ge(S.st_i, 16)

    V.wait_ge(S.a_i, 4)
    V.quantize_mx(T.uq[:], T.us[:], T.ut[:, 8:528]).then_inc(S.q_u, 1)
    for i, done in ((0, S.m_e0), (1, S.m_e1)):
        V.wait_ge(done, 1)
        z = T.pze[:, 512 * i:512 * i + 2]
        V.tensor_scalar(T.ut[:, 2 * i:8:4], z, 0.0, C, AluOpType.max, AluOpType.mult).then_inc(S.a_e, 1)
        V.tensor_scalar(T.ut[:, 2 * i + 1:8:4], z, -C, 0.0, AluOpType.mult, AluOpType.max).then_inc(S.a_e, 1)
    V.wait_ge(S.a_e, 4)
    V.quantize_mx(T.vq[:, B0:B0 + NC], T.vs[:, B0:B0 + NC], T.ut[:, 0:512]).then_inc(S.q_v, 1)
    V.wait_ge(S.m_ye, 1)
    V.tensor_copy(T.ye[:], T.pye[:, 0:4]).then_inc(S.c_e, 1)

    D.wait_ge(S.c_e, 1)
    D.dma_start(T.y[:, 0:4], T.ye[:]).then_inc(S.st_e, 16)
    D.wait_ge(S.st_e, 16)
